import numpy as np
import ml_dtypes


def mxq(x, axis, fmt="e4m3"):
    dtype, down = {"e4m3": (ml_dtypes.float8_e4m3fn, 7), "e5m2": (ml_dtypes.float8_e5m2, 14)}[fmt]
    v = np.moveaxis(np.asarray(x, np.float32).astype(ml_dtypes.bfloat16).astype(np.float64), axis, -1)
    blocks = v.reshape(v.shape[:-1] + (-1, 32))
    amax = np.abs(blocks).max(-1, keepdims=True)
    byte = np.maximum(np.where(amax > 0, np.frexp(amax)[1] - 1 + 127, 0) - down, 1)
    scale = np.exp2(byte - 127.0)
    codes = (blocks / scale).astype(np.float32).astype(dtype).astype(np.float64)
    return np.moveaxis((codes * scale).reshape(v.shape), -1, axis)


WIDE = False


def mx_kscale(k):
    if not WIDE:
        return np.ones(k)
    levels = np.array([30, -30])
    if k % 512:
        return np.exp2(np.random.permutation(np.resize(levels, k // 32))).repeat(32)
    a = np.empty((k // 512, 16))
    for p in range(k // 512):
        a[p, :8] = np.random.permutation(np.resize(levels, 8))
        for g in range(8):
            far = levels[np.abs(levels - a[p, g]) >= 10]
            a[p, g + 8] = far[np.random.randint(len(far))]
    return np.exp2(a.ravel()).repeat(32)


def f64(x):
    return np.asarray(x).astype(np.float64)


def striped(idx):
    return np.tile(np.asarray(idx).reshape(-1, 16).T, (8, 1)).astype(np.uint16)


def unstriped(offs):
    return offs[:16].T.reshape(-1).astype(np.int64)


E2M1 = np.array([0.0, 0.5, 1.0, 1.5, 2.0, 3.0, 4.0, 6.0, -0.0, -0.5, -1.0, -1.5, -2.0, -3.0, -4.0, -6.0])


def pack_weight(w, fmt):
    k, n = w.shape
    w = f64(np.asarray(w, np.float32).astype(ml_dtypes.bfloat16)).reshape(k // 32, 32, n)
    amax = np.abs(w).max(1)
    if fmt in ("e4m3", "e5m2"):
        byte = np.frexp(amax)[1] - 1 + 127 - (7 if fmt == "e4m3" else 14)
    else:
        mant, ex = np.frexp(amax / 6.0)
        byte = np.where(mant > 0.5, ex, ex - 1) + 127
    byte = np.clip(np.where(amax > 0, byte, 1), 1, 254)
    scaled = (w * np.exp2(127.0 - byte)[:, None, :]).reshape(k, n).astype(np.float32)
    by_word = np.ascontiguousarray(scaled.reshape(k // 512, 128, 4, n).transpose(0, 1, 3, 2))
    if fmt in ("e4m3", "e5m2"):
        words = by_word.astype(ml_dtypes.float8_e4m3fn if fmt == "e4m3" else ml_dtypes.float8_e5m2).view(np.uint8)
    else:
        c = by_word.astype(ml_dtypes.float4_e2m1fn).view(np.uint8) & 0xF
        words = (c[..., 0::2] | (c[..., 1::2] << 4)).reshape(k // 512, 128, 2 * n)
    return np.ascontiguousarray(words), np.ascontiguousarray(byte.astype(np.uint8).reshape(k // 512, 16, n))


def unpack_weight(words, scales, fmt):
    g, _, n = scales.shape
    words = np.ascontiguousarray(words).reshape(g, 128, n, -1)
    if fmt in ("e4m3", "e5m2"):
        vals = words.view(ml_dtypes.float8_e4m3fn if fmt == "e4m3" else ml_dtypes.float8_e5m2).astype(np.float64)
    else:
        nib = np.empty((g, 128, n, 4), np.uint8)
        nib[..., 0::2] = words & 0xF
        nib[..., 1::2] = words >> 4
        vals = E2M1[nib]
    vals = vals * np.repeat(np.exp2(scales.astype(np.float64) - 127.0), 8, axis=1)[..., None]
    return vals.transpose(0, 1, 3, 2).reshape(g * 512, n)


def sgn(shape):
    return np.random.uniform(0.5, 2.0, shape) * np.where(np.random.standard_normal(shape) < 0, -1.0, 1.0)


K, T, J, R, C, O, N, E = 512, 1024, 256, 512, 512, 128, 256, 1024


def setup_inputs():
    n = np.random.standard_normal
    idx = np.random.permutation(T)[:J]
    idx2 = np.random.permutation(C)[:J]
    idx3 = np.random.permutation(C)[:O]
    idx4 = np.random.permutation(C)[:O]
    idx5 = np.random.permutation(J)[:O]
    idx6 = np.random.permutation(T)[:O]
    idx7 = np.random.permutation(E)[:O]
    fk = mx_kscale(K)
    fr = mx_kscale(R)
    xtp = pack_weight(n((K, T)) / fk[:, None], "e2m1")
    wp = pack_weight(n((K, R)) * 1 / np.sqrt(K) * fk[:, None], "e5m2")
    w2p = pack_weight(n((K, R)) * 1 / np.sqrt(K) * fk[:, None], "e4m3")
    wbp = pack_weight(n((R, N)) * 1 / np.sqrt(R) / fr[:, None], "e4m3")
    wsp = pack_weight(n((K, N)) * 1 / np.sqrt(K) * fk[:, None], "e4m3")
    return {
        "xt_words": xtp[0],
        "xt_scales": xtp[1],
        "w_words": wp[0],
        "w_scales": wp[1],
        "w2_words": w2p[0],
        "w2_scales": w2p[1],
        "sa": (sgn((R, 1)) * fr[:, None]).astype(np.float32),
        "sb": (np.random.uniform(0.5, 1.6, (R, 1)) * fr[:, None]).astype(np.float32),
        "wb_words": wbp[0],
        "wb_scales": wbp[1],
        "ws_words": wsp[0],
        "ws_scales": wsp[1],
        "offs": striped(idx),
        "offs2": striped(idx2),
        "offs3": striped(idx3),
        "offs4": striped(idx4),
        "offs5": striped(idx5),
        "offs6": striped(idx6),
        "offs7": striped(idx7),
    }


def reference(xt_words, xt_scales, w_words, w_scales, w2_words, w2_scales, sa, sb, wb_words, wb_scales, ws_words, ws_scales, offs, offs2, offs3, offs4, offs5, offs6, offs7):
    idx = unstriped(offs)
    idx2 = unstriped(offs2)
    idx3 = unstriped(offs3)
    idx4 = unstriped(offs4)
    idx5 = unstriped(offs5)
    idx6 = unstriped(offs6)
    idx7 = unstriped(offs7)
    xtu = unpack_weight(xt_words, xt_scales, "e2m1")
    wu = unpack_weight(w_words, w_scales, "e5m2")
    w2u = unpack_weight(w2_words, w2_scales, "e4m3")
    wbu = unpack_weight(wb_words, wb_scales, "e4m3")
    wsu = unpack_weight(ws_words, ws_scales, "e4m3")
    xtidxg = xtu[:, idx]
    a = wu.T @ xtidxg
    b = w2u.T @ xtidxg
    pw = np.zeros((R, C))
    pw[:, idx2] = a
    nm = -np.max(pw, axis=1, keepdims=True)
    hid = np.maximum(pw[:, idx3] * f64(sa) * np.exp(pw[:, idx4] + nm), b[:, idx5] * f64(sb))
    hidq = mxq(hid, 0, "e5m2")
    xtidx6g = xtu[:, idx6]
    p = wbu.T @ hidq + wsu.T @ xtidx6g
    y = np.zeros((N, E))
    y[:, idx7] = p
    return y

from contextlib import ExitStack

import concourse.mybir as mybir

F32 = mybir.dt.float32
BF16 = mybir.dt.bfloat16
I32 = mybir.dt.int32
U32 = mybir.dt.uint32
U16 = mybir.dt.uint16
U8 = mybir.dt.uint8
E2M1 = mybir.dt.float4_e2m1fn_x4
E4M3 = mybir.dt.float8_e4m3fn_x4
E5M2 = mybir.dt.float8_e5m2_x4
ALU = mybir.AluOpType
ACT = mybir.ActivationFunctionType

K, T, J, R, C, O, N, E = 512, 1024, 256, 512, 512, 128, 256, 1024
P = 128
PACK = 4
QUAD = 32
FLOPS = 2 * (2 * K * R * J + R * N * O + K * N * O)


def tile_list_fadedread_twow_further_scattered_kernel(
    tc, xt_words, xt_scales, w_words, w_scales, w2_words, w2_scales, sa, sb,
    wb_words, wb_scales, ws_words, ws_scales,
    offs, offs2, offs3, offs4, offs5, offs6, offs7, out,
):
    nc = tc.nc
    with ExitStack() as ctx:
        lists = ctx.enter_context(tc.tile_pool(name="lists", bufs=1))
        sbuf = ctx.enter_context(tc.tile_pool(name="sbuf", bufs=1))
        psum = ctx.enter_context(tc.psum_pool(name="psum", bufs=1))

        def load_list(src, name):
            t = lists.tile(list(src.shape), U16, name=name)
            nc.sync.dma_start(out=t[:], in_=src)
            return t

        def load_scale_rows(plane, scales):
            rows = scales[0].rearrange("(q r) c -> r q c", r=PACK)
            for r in range(PACK):
                nc.sync.dma_start(out=plane[r:P:QUAD, :].bitcast(I32), in_=rows[r].bitcast(I32))

        def load_words(queue, words, width, name, tag):
            t = sbuf.tile([P, width], I32, name=name, tag=tag, align_bytes=64)
            queue.dma_start(out=t[:], in_=words[0].rearrange("p c t -> p (c t)").bitcast(I32))
            return t

        def deal_words(copy, raw, name, parts):
            tiles = []
            n = PACK // parts
            for u in range(parts):
                t = sbuf.tile([P, n, P], U32, name="%s%d" % (name, u), tag="%s%d" % (name, u), align_bytes=64)
                copy(
                    out=t[:].rearrange("p t (c i) -> p c t i", i=4),
                    in_=raw[:].bitcast(U32).rearrange("p (c i t) -> p c t i", i=4, t=PACK)[:, :, u * n : (u + 1) * n, :],
                )
                tiles.extend(t[:, v, :] for v in range(n))
            return tiles

        def deal_scales(engine, plane, name):
            t = sbuf.tile([P, PACK, P], U8, name=name, tag=name, align_bytes=64)
            engine.tensor_copy(
                out=t[:].rearrange("p t (c i) -> p c t i", i=16),
                in_=plane.rearrange("p (c i t) -> p c t i", i=16, t=PACK),
            )
            return t

        xs_plane = sbuf.tile([P, T], U8, name="xs_plane", align_bytes=64)
        nc.gpsimd.memset(xs_plane[:].bitcast(I32), 0)
        planes = sbuf.tile([P, R + 2 * N], U8, name="planes", align_bytes=64)
        nc.vector.memset(planes[:].bitcast(I32), 0)
        w_plane, ws_plane, wb_plane = planes[:, 0:R], planes[:, R : R + N], planes[:, R + N : R + 2 * N]
        w2_plane = sbuf.tile([P, R], U8, name="w2_plane", tag="w2_plane", align_bytes=64)
        nc.vector.memset(w2_plane[:].bitcast(I32), 0)

        l1 = load_list(offs, "l1")
        xw = sbuf.tile([P, T], U16, name="xw", align_bytes=64)
        nc.scalar.dma_start(out=xw[:].bitcast(I32), in_=xt_words[0].bitcast(I32))
        w_stage = sbuf.tile([PACK, PACK, R // 4], I32, name="w_stage")
        nc.sync.dma_start(out=w_stage[:], in_=w_scales[0].rearrange("(q r) c -> r q c", r=PACK).bitcast(I32))
        w_raw = load_words(nc.scalar, w_words, R, "w_raw", "w_raw")
        load_scale_rows(xs_plane, xt_scales)
        l6 = load_list(offs6, "l6")
        w2_raw = load_words(nc.sync, w2_words, R, "w2_raw", "w2_raw")
        l2 = load_list(offs2, "l2")
        load_scale_rows(w2_plane, w2_scales)
        l4 = load_list(offs4, "l4")
        l3 = load_list(offs3, "l3")
        sa_t = sbuf.tile([P, PACK], F32, name="sa_t")
        nc.sync.dma_start(out=sa_t[:], in_=sa.rearrange("(p t) o -> p (t o)", t=PACK))
        l5 = load_list(offs5, "l5")
        sb_t = sbuf.tile([P, PACK], F32, name="sb_t")
        nc.sync.dma_start(out=sb_t[:], in_=sb.rearrange("(p t) o -> p (t o)", t=PACK))
        ws_w = load_words(nc.sync, ws_words, N, "ws_w", "ws_w")
        load_scale_rows(ws_plane, ws_scales)
        wb_w = load_words(nc.sync, wb_words, N, "wb_w", "wb_w")
        load_scale_rows(wb_plane, wb_scales)
        l7 = load_list(offs7, "l7")

        boards = []
        for t in range(PACK):
            board = sbuf.tile([P, C], F32, name="board%d" % t)
            nc.vector.memset(board[:], 0.0)
            boards.append(board)
        page0 = sbuf.tile([P, E], F32, name="page0")
        nc.vector.memset(page0[:], 0.0)

        for q in range(PACK):
            nc.vector.tensor_copy(out=w_plane[QUAD * q : QUAD * q + PACK, :].bitcast(I32), in_=w_stage[:, q, :])
        w_sc = deal_scales(nc.gpsimd, w_plane, "w_sc")
        w_cd = deal_words(nc.scalar.copy, w_raw, "w_cd", 2)

        xg = sbuf.tile([P, J], U16, name="xg", align_bytes=64)
        xg_sc = sbuf.tile([P, J], U8, name="xg_sc", align_bytes=64)
        nc.vector.tensor_copy(out=xg[:], in_=xw[:].indirect(l1[:]))
        nc.vector.tensor_copy(out=xg_sc[:], in_=xs_plane[:].indirect(l1[:]))

        x6 = sbuf.tile([P, O], U16, name="x6", align_bytes=64)
        x6_sc = sbuf.tile([P, O], U8, name="x6_sc", align_bytes=64)
        nc.vector.tensor_copy(out=x6[:], in_=xw[:].indirect(l6[:]))
        nc.vector.tensor_copy(out=x6_sc[:], in_=xs_plane[:].indirect(l6[:]))

        w2_cd = deal_words(nc.gpsimd.tensor_copy, w2_raw, "w2_cd", 1)
        w2_sc = deal_scales(nc.gpsimd, w2_plane[:], "w2_sc")

        page1 = sbuf.tile([P, E], F32, name="page1", tag="w2_plane", align_bytes=64)
        nc.gpsimd.memset(page1[:], 0.0)
        pages = [page0, page1]

        a_ps = [psum.tile([P, J], F32, name="a_ps%d" % t) for t in range(PACK)]
        b_ps = [psum.tile([P, 2, J], F32, name="b_ps%d" % u, tag="late%d" % u) for u in range(2)]
        for t in range(PACK):
            nc.tensor.matmul_mx(out=a_ps[t][:], lhsT=w_cd[t].bitcast(E5M2), lhsT_scale=w_sc[:, t, :],
                                rhs=xg[:].bitcast(E2M1), rhs_scale=xg_sc[:], start=True, stop=True)
        for t in range(PACK):
            nc.tensor.matmul_mx(out=b_ps[t // 2][:, t % 2, :], lhsT=w2_cd[t].bitcast(E4M3), lhsT_scale=w2_sc[:, t, :],
                                rhs=xg[:].bitcast(E2M1), rhs_scale=xg_sc[:], start=True, stop=True)

        top = sbuf.tile([P, PACK], F32, name="top")
        nm = sbuf.tile([P, PACK], F32, name="nm")
        a_sb = [sbuf.tile([P, J], F32, name="a_sb%d" % t, tag="a_sb%d" % t, align_bytes=64) for t in range(PACK)]
        b_sb = [sbuf.tile([P, J], F32, name="b_sb%d" % t) for t in range(PACK)]
        for t in range(PACK):
            nc.vector.tensor_scalar(out=a_sb[t][:], in0=a_ps[t][:], scalar1=1.0, scalar2=0.0,
                                    op0=ALU.mult, op1=ALU.max, accum_out=top[:, t : t + 1])
        nc.vector.tensor_scalar(out=nm[:], in0=top[:], scalar1=-1.0, scalar2=None, op0=ALU.mult)

        picked = sbuf.tile([P, PACK, O], F32, name="picked")
        faded = sbuf.tile([P, PACK, O], F32, name="faded")
        second = [sbuf.tile([P, PACK, O // 2], F32, name="second%d" % g) for g in range(2)]
        prod = sbuf.tile([P, PACK, O], F32, name="prod", tag="w2_cd0", align_bytes=64)

        def look_board(t):
            nc.scalar.activation(out=picked[:, t, :], in_=boards[t][:].indirect(l3[:]), func=ACT.Copy, scale=sa_t[:, t : t + 1])
            nc.scalar.activation(out=faded[:, t, :], in_=boards[t][:].indirect(l4[:]), func=ACT.Exp, bias=nm[:, t : t + 1])

        def look_second(t, g):
            nc.scalar.activation(out=second[g][:, t, :], in_=b_sb[t][:].indirect(l5[:, 4 * g : 4 * g + 4]),
                                 func=ACT.Copy, scale=sb_t[:, t : t + 1])

        def multiply(t):
            nc.vector.tensor_tensor(out=prod[:, t, :], in0=picked[:, t, :], in1=faded[:, t, :], op=ALU.mult)

        for u in range(2):
            nc.scalar.activation(out=boards[2 * u][:].indirect(l2[:]), in_=a_sb[2 * u][:], func=ACT.Copy)
        for u in range(2):
            nc.vector.tensor_copy(out=boards[2 * u + 1][:].indirect(l2[:]), in_=a_sb[2 * u + 1][:])
        for t in range(PACK):
            nc.vector.tensor_copy(out=b_sb[t][:], in_=b_ps[t // 2][:, t % 2, :])
        for t in range(PACK):
            look_board(t)
        for g in range(2):
            for t in range(PACK):
                look_second(t, g)

        p_ps = [psum.tile([P, O], F32, name="p_ps%d" % h, tag="late%d" % h) for h in range(N // P)]
        for h in range(N // P):
            cols = slice(h * P, (h + 1) * P)
            nc.tensor.matmul_mx(out=p_ps[h][:], lhsT=ws_w[:, cols].bitcast(E4M3), lhsT_scale=ws_plane[:, cols],
                                rhs=x6[:].bitcast(E2M1), rhs_scale=x6_sc[:], start=True, stop=False)

        for t in range(PACK):
            multiply(t)
        hid_cd = sbuf.tile([P, O], U32, name="hid_cd", align_bytes=64)
        hid_sc = sbuf.tile([P, O], U8, name="hid_sc", align_bytes=64)
        for g in range(2):
            cols = slice(g * O // 2, (g + 1) * O // 2)
            hid = sbuf.tile([P, O // 2, PACK], BF16, name="hid%d" % g, align_bytes=64)
            nc.vector.tensor_tensor(
                out=hid[:].rearrange("p (c i) t -> p c t i", i=4),
                in0=prod[:, :, cols].rearrange("p t (c i) -> p c t i", i=4),
                in1=second[g][:].rearrange("p t (c i) -> p c t i", i=4),
                op=ALU.max,
            )
            nc.vector.quantize_mx(out=hid_cd[:, cols].bitcast(E5M2), scales=hid_sc[:, cols], in_=hid[:].rearrange("p o t -> p (o t)"))

        for h in range(N // P):
            cols = slice(h * P, (h + 1) * P)
            nc.tensor.matmul_mx(out=p_ps[h][:], lhsT=wb_w[:, cols].bitcast(E4M3), lhsT_scale=wb_plane[:, cols],
                                rhs=hid_cd[:].bitcast(E5M2), rhs_scale=hid_sc[:], start=False, stop=True)
        p_sb = [sbuf.tile([P, O], F32, name="p_sb%d" % h) for h in range(N // P)]
        nc.vector.tensor_copy(out=p_sb[0][:], in_=p_ps[0][:])
        nc.vector.tensor_copy(out=pages[0][:].indirect(l7[:]), in_=p_sb[0][:])
        nc.sync.dma_start(out=out[0:P, :], in_=pages[0][:])
        nc.scalar.copy(out=p_sb[1][:], in_=p_ps[1][:])
        nc.scalar.activation(out=pages[1][:].indirect(l7[:]), in_=p_sb[1][:], func=ACT.Copy)
        nc.scalar.dma_start(out=out[P : 2 * P, :], in_=pages[1][:])
